import numpy as np
import ml_dtypes


def mxq(x, axis, fmt="e4m3"):
    dtype, down = {"e4m3": (ml_dtypes.float8_e4m3fn, 7), "e5m2": (ml_dtypes.float8_e5m2, 14)}[fmt]
    v = np.moveaxis(np.asarray(x, np.float32).astype(ml_dtypes.bfloat16).astype(np.float64), axis, -1)
    blocks = v.reshape(v.shape[:-1] + (-1, 32))
    amax = np.abs(blocks).max(-1, keepdims=True)
    byte = np.maximum(np.where(amax > 0, np.frexp(amax)[1] - 1 + 127, 0) - down, 1)
    scale = np.exp2(byte - 127.0)
    codes = (blocks / scale).astype(np.float32).astype(dtype).astype(np.float64)
    return np.moveaxis((codes * scale).reshape(v.shape), -1, axis)


WIDE = False


def mx_kscale(k):
    if not WIDE:
        return np.ones(k)
    levels = np.array([10, -10, 5, -5, 0])
    if k % 512:
        return np.exp2(np.random.permutation(np.resize(levels, k // 32))).repeat(32)
    a = np.empty((k // 512, 16))
    for p in range(k // 512):
        a[p, :8] = np.random.permutation(np.resize(levels, 8))
        for g in range(8):
            far = levels[np.abs(levels - a[p, g]) >= 10]
            a[p, g + 8] = far[np.random.randint(len(far))]
    return np.exp2(a.ravel()).repeat(32)


def f64(x):
    return np.asarray(x).astype(np.float64)


def striped(idx):
    return np.tile(idx.reshape(-1, 16).T, (8, 1)).astype(np.uint16)


def unstriped(offs):
    return offs[:16].T.reshape(-1).astype(np.int64)


def striped8(idx):
    return np.concatenate([x.reshape(-1, 16).T for x in idx]).astype(np.uint16)


def runs(offs, k):
    lists = np.stack([offs[16 * r : 16 * r + 16].T.reshape(-1) for r in range(8)]).astype(np.int64)
    return lists[np.arange(k) % 512 // 64]


def pack_weight(w):
    k, n = w.shape
    w = f64(np.asarray(w, np.float32).astype(ml_dtypes.bfloat16)).reshape(k // 32, 32, n)
    amax = np.abs(w).max(1)
    byte = np.clip(np.where(amax > 0, np.frexp(amax)[1] - 1 + 127 - 7, 1), 1, 254)
    scaled = (w * np.exp2(127.0 - byte)[:, None, :]).reshape(k, n).astype(np.float32)
    words = np.ascontiguousarray(scaled.reshape(k // 512, 128, 4, n).transpose(0, 1, 3, 2)).astype(ml_dtypes.float8_e4m3fn).view(np.uint8)
    return words, np.ascontiguousarray(byte.astype(np.uint8).reshape(k // 512, 16, n))


def unpack_weight(words, scales):
    g, p, n, _ = words.shape
    vals = np.ascontiguousarray(words).view(ml_dtypes.float8_e4m3fn).astype(np.float64) * np.repeat(np.exp2(scales.astype(np.float64) - 127.0), 8, axis=1)[..., None]
    return vals.transpose(0, 1, 3, 2).reshape(g * 512, n)


def sigmoid(v):
    return 1.0 / (1.0 + np.exp(-np.maximum(v, -700.0)))


K, T, S, H, G = 512, 1024, 512, 512, 2048


def setup_inputs():
    n = np.random.standard_normal
    s = mx_kscale(K)[:, None]
    packed_xT = pack_weight(n((K, T)) * s)
    packed_dT = pack_weight(n((K, G)) / s)
    return {
        "x_words": packed_xT[0],
        "x_scales": packed_xT[1],
        "w1": (n((K, H)) / np.sqrt(K) / s).astype(np.float32),
        "w2": (n((K, H)) / np.sqrt(K) / s).astype(np.float32),
        "gs": (np.random.uniform(0.5, 1.5, (K, 1)) * s).astype(np.float32),
        "d_words": packed_dT[0],
        "d_scales": packed_dT[1],
        "offs": striped(np.random.permutation(T)[:S]),
        "two": striped(np.random.permutation(T)[:S]),
        "n1": striped8(np.stack([np.random.permutation(S) for _ in range(8)])),
        "n2": striped8(np.stack([np.random.permutation(S) for _ in range(8)])),
        "k1": striped8(np.random.randint(0, G, (8, H))),
        "n3": striped8(np.stack([np.random.permutation(S) for _ in range(8)])),
        "n4": striped8(np.stack([np.random.permutation(S) for _ in range(8)])),
    }


def reference(x_words, x_scales, w1, w2, gs, d_words, d_scales, offs, two, n1, n2, k1, n3, n4):
    d_k1 = unpack_weight(d_words, d_scales)[np.arange(K)[:, None], runs(k1, K)]
    xq = unpack_weight(x_words, x_scales)[:, unstriped(offs)]
    y = mxq(f64(w1), 0, "e4m3").T @ xq
    x_two = unpack_weight(x_words, x_scales)[:, unstriped(two)]
    d = mxq(f64(w2), 0, "e4m3").T @ x_two
    z = f64(gs) * (y + (sigmoid(d[np.arange(H)[:, None], runs(n2, H)] - d)) * (y[np.arange(H)[:, None], runs(n1, H)] - y))
    h = 0.0625 * ((d_k1.T @ mxq(z, 0, "e4m3")))
    return (h * (h[np.arange(H)[:, None], runs(n3, H)])) * (np.tanh(h[np.arange(H)[:, None], runs(n4, H)]))

@@ -1,0 +1,240 @@
+import math
+from contextlib import ExitStack
+
+import concourse.mybir as mybir
+
+K, T, S, H, G = 512, 1024, 512, 512, 2048
+FLOPS = 3 * 2 * K * H * S
+
+F32 = mybir.dt.float32
+BF16 = mybir.dt.bfloat16
+I32 = mybir.dt.int32
+U32 = mybir.dt.uint32
+U16 = mybir.dt.uint16
+U8 = mybir.dt.uint8
+FP8X4 = mybir.dt.float8_e4m3fn_x4
+ACT = mybir.ActivationFunctionType
+ALU = mybir.AluOpType
+
+P = 128
+PACK = 4
+HALF = S // 2
+WINDOW = 2 * S
+
+
+def tile_picked_twqpullbcube_none_p_kernel(
+    tc, x_words, x_scales, w1, w2, gs, d_words, d_scales, offs, two, n1, n2, k1, n3, n4, out
+):
+    nc = tc.nc
+    with ExitStack() as ctx:
+        held = ctx.enter_context(tc.tile_pool(name="held", bufs=1))
+        psum = ctx.enter_context(tc.psum_pool(name="psum", bufs=1))
+
+        def sb(shape, dtype, name):
+            return held.tile(shape, dtype, name=name, align_bytes=64)
+
+        def load_list(src, name):
+            lst = sb([P, S // 16], U16, name)
+            nc.sync.dma_start(lst[:], src)
+            return lst
+
+        def load_weight(w, name):
+            halves = []
+            for c in range(2):
+                raw = sb([P, PACK, H // 2], F32, f"{name}_raw{c}")
+                nc.sync.dma_start(raw[:], w[:, c * (H // 2) : (c + 1) * (H // 2)].rearrange("(p j) c -> p j c", j=PACK))
+                halves.append(raw)
+            return halves
+
+        xs = sb([P, T], U8, "xs")
+        nc.vector.memset(xs[:].bitcast(I32), 0)
+        ds = sb([P, G], U8, "ds")
+        nc.vector.memset(ds[:].bitcast(I32), 0)
+        dq_scales = sb([P, H], U8, "dq_scales")
+        nc.vector.memset(dq_scales[:].bitcast(I32), 0)
+        win_d = [sb([P, WINDOW], F32, f"win_d{t}") for t in range(PACK)]
+        win_y = [sb([P, WINDOW], F32, f"win_y{t}") for t in range(PACK)]
+        for t in range(PACK):
+            nc.vector.memset(win_d[t][:, S:WINDOW], 0.0)
+        warm = sb([P, 8], F32, "warm")
+        nc.scalar.activation(warm[:, 0:1], win_d[0][:, S : S + 1], ACT.Sigmoid)
+
+        l_two = load_list(two, "l_two")
+        xw = sb([P, T], U32, "xw")
+        nc.sync.dma_start(xw[:].bitcast(I32), x_words[0].rearrange("p n t -> p (n t)").bitcast(I32))
+        for q in range(4):
+            nc.scalar.dma_start(xs[32 * q : 32 * q + 4, :].bitcast(I32), x_scales[0][4 * q : 4 * q + 4, :].bitcast(I32))
+        l_offs = load_list(offs, "l_offs")
+        w2_raw = load_weight(w2, "w2")
+        l_n2 = load_list(n2, "l_n2")
+        l_k1 = load_list(k1, "l_k1")
+        nc.sync.dma_start(ds[0:P:8, :].bitcast(I32), d_scales[0].bitcast(I32))
+        dw = sb([P, G], U32, "dw")
+        nc.sync.dma_start(dw[:].bitcast(I32), d_words[0].rearrange("p n t -> p (n t)").bitcast(I32))
+        w1_raw = load_weight(w1, "w1")
+        gain = sb([P, PACK], F32, "gain")
+        nc.sync.dma_start(gain[:], gs.rearrange("(p t) o -> p (t o)", t=PACK))
+        l_n1 = load_list(n1, "l_n1")
+        l_n3 = load_list(n3, "l_n3")
+        l_n4 = load_list(n4, "l_n4")
+
+        def pick_words(table, lst, name):
+            got = sb([P, S], U32, name)
+            nc.vector.tensor_copy(got[:], table[:].indirect(lst[:]))
+            return got
+
+        def pick_bytes(table, lst, name):
+            got = sb([P, S], U8, name)
+            nc.vector.tensor_copy(got[:], table[:].indirect(lst[:]))
+            return got
+
+        def cast_weight(raw, name):
+            wb = sb([P, PACK, P, PACK], BF16, name)
+            for c in range(2):
+                nc.scalar.copy(
+                    wb[:, :, c * 64 : (c + 1) * 64, :].rearrange("p t m j -> p m j t"),
+                    raw[c][:].rearrange("p j (m t) -> p m j t", t=PACK),
+                )
+            return wb
+
+        def quantize(src, width, name):
+            codes = sb([P, width], U32, name + "_codes")
+            scales = sb([P, width], U8, name + "_scales")
+            nc.vector.quantize_mx(out=codes[:].bitcast(FP8X4), scales=scales[:], in_=src)
+            return codes, scales
+
+        def product(bank, width, lhs, t, rhs, name):
+            acc = psum.tile([P, width], F32, name=name, tag=f"bank{bank}")
+            cols = slice(t * P, (t + 1) * P)
+            nc.tensor.matmul_mx(
+                out=acc[:],
+                lhsT=lhs[0][:, cols].bitcast(FP8X4),
+                lhsT_scale=lhs[1][:, cols],
+                rhs=rhs[0][:].bitcast(FP8X4),
+                rhs_scale=rhs[1][:],
+                start=True,
+                stop=True,
+            )
+            return acc
+
+        x2w = pick_words(xw, l_two, "x2w")
+        x1w = pick_words(xw, l_offs, "x1w")
+        x2s = pick_bytes(xs, l_two, "x2s")
+        w2b = cast_weight(w2_raw, "w2b")
+        w2q = quantize(w2b[:].rearrange("p t m j -> p (t m j)"), H, "w2q")
+        x1s = pick_bytes(xs, l_offs, "x1s")
+        d_acc = [product(t, S, w2q, t, (x2w, x2s), f"d_acc{t}") for t in range(PACK)]
+
+        def evac_d(t, by_dma):
+            nc.scalar.copy(win_d[t][:, 0:S], d_acc[t][:])
+            if by_dma:
+                nc.sync.dma_start(win_y[t][:, S:WINDOW], win_d[t][:, 0:S])
+            else:
+                nc.scalar.copy(win_y[t][:, S:WINDOW], d_acc[t][:])
+
+        diff = [sb([P, S], F32, f"diff{t}") for t in range(PACK)]
+        gate = [sb([P, S], F32, f"gate{t}") for t in range(PACK)]
+
+        def pull_d(t):
+            nc.vector.tensor_tensor(diff[t][:], win_d[t][:].indirect(l_n2[:]), win_y[t][:, S:WINDOW], ALU.subtract)
+
+        dg_bytes = pick_bytes(ds, l_k1, "dg_bytes")
+        dg_words = pick_words(dw, l_k1, "dg_words")
+        evac_d(0, False)
+        evac_d(2, True)
+        evac_d(3, True)
+        evac_d(1, False)
+        w1b = cast_weight(w1_raw, "w1b")
+        dealt_bytes = sb([P, H], U8, "dealt_bytes")
+        nc.vector.tensor_copy(
+            dealt_bytes[:].bitcast(I32).rearrange("p (t a) -> p a t", t=PACK),
+            dg_bytes[:].bitcast(I32).rearrange("p (a t) -> p a t", t=PACK),
+        )
+        dq_words = sb([P, H], U32, "dq_words")
+        nc.vector.tensor_copy(
+            dq_words[:].rearrange("p (t a b) -> p a t b", t=PACK, b=4),
+            dg_words[:].rearrange("p (a t b) -> p a t b", t=PACK, b=4),
+        )
+        for r in range(4):
+            nc.sync.dma_start(dq_scales[r:P:32, :].bitcast(I32), dealt_bytes[8 * r : P : 32, :].bitcast(I32))
+        pull_d(0)
+        pull_d(1)
+        pull_d(2)
+        w1q = quantize(w1b[:].rearrange("p t m j -> p (t m j)"), H, "w1q")
+        y_acc = [product(4 + t, S, w1q, t, (x1w, x1s), f"y_acc{t}") for t in range(PACK)]
+        pull_d(3)
+
+        for t in range(PACK):
+            nc.scalar.activation(gate[t][:], diff[t][:], ACT.Sigmoid)
+            nc.scalar.activation(win_y[t][:, 0:S], y_acc[t][:], ACT.Copy, scale=gain[:, t : t + 1])
+
+        far = [sb([P, PACK, HALF], F32, f"far{c}") for c in range(2)]
+        near = [sb([P, PACK, HALF], F32, f"near{c}") for c in range(2)]
+
+        def far_part(t, c):
+            cols = slice(c * HALF, (c + 1) * HALF)
+            nc.vector.tensor_tensor(
+                far[c][:, t, :], win_y[t][:].indirect(l_n1[:, c * 16 : (c + 1) * 16]), gate[t][:, cols], ALU.mult
+            )
+
+        def near_part(t, c):
+            cols = slice(c * HALF, (c + 1) * HALF)
+            nc.vector.scalar_tensor_tensor(
+                near[c][:, t, :], gate[t][:, cols], 1.0, win_y[t][:, cols], ALU.subtract, ALU.mult
+            )
+
+        zb = [sb([P, HALF * PACK], BF16, f"zb{c}") for c in range(2)]
+
+        def join(c):
+            nc.vector.tensor_tensor(
+                zb[c][:].rearrange("p (g i t) -> p g t i", i=4, t=PACK),
+                far[c][:].rearrange("p t (g i) -> p g t i", i=4),
+                near[c][:].rearrange("p t (g i) -> p g t i", i=4),
+                ALU.subtract,
+            )
+
+        h_again = [sb([P, S], F32, f"h_again{t}") for t in range(PACK)]
+        alpha = math.sqrt(2.0) / 16.0
+        beta = math.sqrt(2.0)
+
+        def second_product(c, zq):
+            cols = slice(c * HALF, (c + 1) * HALF)
+            for t in range(PACK):
+                acc = product(2 * t + c, HALF, (dq_words, dq_scales), t, zq, f"h_acc{t}_{c}")
+                nc.scalar.activation(win_d[t][:, cols], acc[:], ACT.Copy, scale=alpha)
+                nc.scalar.activation(h_again[t][:, cols], acc[:], ACT.Copy, scale=alpha)
+                if c == 1:
+                    finish(t)
+
+        out_rows = out.rearrange("(a t b) n -> t a b n", t=PACK, b=4)
+
+        def finish(t):
+            sig = sb([P, S], F32, f"sig{t}")
+            nc.scalar.activation(sig[:], win_d[t][:].indirect(l_n4[:]), ACT.Sigmoid, scale=beta)
+            pair = sb([P, S], F32, f"pair{t}")
+            nc.vector.tensor_tensor(pair[:], win_d[t][:].indirect(l_n3[:]), h_again[t][:], ALU.mult)
+            pieces = 2 if t == PACK - 1 else 1
+            width = S // pieces
+            for c in range(pieces):
+                cols = slice(c * width, (c + 1) * width)
+                res = sb([P, width], F32, f"res{t}_{c}")
+                nc.vector.scalar_tensor_tensor(res[:], sig[:, cols], 0.5, pair[:, cols], ALU.subtract, ALU.mult)
+                nc.sync.dma_start(out_rows[t][:, :, cols], res[:])
+
+        for c in range(2):
+            far_part(0, c)
+            near_part(0, c)
+        for t in range(1, PACK):
+            far_part(t, 0)
+            near_part(t, 0)
+        join(0)
+        far_part(1, 1)
+        zq0 = quantize(zb[0][:], HALF, "zq0")
+        second_product(0, zq0)
+        near_part(1, 1)
+        for t in range(2, PACK):
+            far_part(t, 1)
+            near_part(t, 1)
+        join(1)
+        zq1 = quantize(zb[1][:], HALF, "zq1")
+        second_product(1, zq1)

@@ -38,40 +38,38 @@ def tile_picked_twqpullbcube_none_p_kernel(
             nc.sync.dma_start(lst[:], src)
             return lst
 
-        def load_weight(w, name):
-            halves = []
-            for c in range(2):
-                raw = sb([P, PACK, H // 2], F32, f"{name}_raw{c}")
-                nc.sync.dma_start(raw[:], w[:, c * (H // 2) : (c + 1) * (H // 2)].rearrange("(p j) c -> p j c", j=PACK))
-                halves.append(raw)
-            return halves
+        def load_weight_half(w, c, name):
+            raw = sb([P, PACK, H // 2], F32, name)
+            nc.sync.dma_start(raw[:], w[:, c * (H // 2) : (c + 1) * (H // 2)].rearrange("(p j) c -> p j c", j=PACK))
+            return raw
 
         xs = sb([P, T], U8, "xs")
-        nc.vector.memset(xs[:].bitcast(I32), 0)
+        nc.gpsimd.memset(xs[:].bitcast(I32), 0)
         ds = sb([P, G], U8, "ds")
-        nc.vector.memset(ds[:].bitcast(I32), 0)
+        nc.gpsimd.memset(ds[:].bitcast(I32), 0)
         dq_scales = sb([P, H], U8, "dq_scales")
-        nc.vector.memset(dq_scales[:].bitcast(I32), 0)
+        nc.gpsimd.memset(dq_scales[:].bitcast(I32), 0)
         win_d = [sb([P, WINDOW], F32, f"win_d{t}") for t in range(PACK)]
         win_y = [sb([P, WINDOW], F32, f"win_y{t}") for t in range(PACK)]
         for t in range(PACK):
-            nc.vector.memset(win_d[t][:, S:WINDOW], 0.0)
+            (nc.vector if t < 2 else nc.gpsimd).memset(win_d[t][:, S:WINDOW], 0.0)
         warm = sb([P, 8], F32, "warm")
         nc.scalar.activation(warm[:, 0:1], win_d[0][:, S : S + 1], ACT.Sigmoid)
 
         l_two = load_list(two, "l_two")
+        for q in range(4):
+            nc.sync.dma_start(xs[32 * q : 32 * q + 4, :].bitcast(I32), x_scales[0][4 * q : 4 * q + 4, :].bitcast(I32))
+        l_offs = load_list(offs, "l_offs")
         xw = sb([P, T], U32, "xw")
         nc.sync.dma_start(xw[:].bitcast(I32), x_words[0].rearrange("p n t -> p (n t)").bitcast(I32))
-        for q in range(4):
-            nc.scalar.dma_start(xs[32 * q : 32 * q + 4, :].bitcast(I32), x_scales[0][4 * q : 4 * q + 4, :].bitcast(I32))
-        l_offs = load_list(offs, "l_offs")
-        w2_raw = load_weight(w2, "w2")
-        l_n2 = load_list(n2, "l_n2")
+        w2_raw = [load_weight_half(w2, c, f"w2_raw{c}") for c in range(2)]
+        w1_raw = [load_weight_half(w1, 0, "w1_raw0")]
         l_k1 = load_list(k1, "l_k1")
         nc.sync.dma_start(ds[0:P:8, :].bitcast(I32), d_scales[0].bitcast(I32))
         dw = sb([P, G], U32, "dw")
         nc.sync.dma_start(dw[:].bitcast(I32), d_words[0].rearrange("p n t -> p (n t)").bitcast(I32))
-        w1_raw = load_weight(w1, "w1")
+        w1_raw.append(load_weight_half(w1, 1, "w1_raw1"))
+        l_n2 = load_list(n2, "l_n2")
         gain = sb([P, PACK], F32, "gain")
         nc.sync.dma_start(gain[:], gs.rearrange("(p t) o -> p (t o)", t=PACK))
         l_n1 = load_list(n1, "l_n1")
@@ -88,49 +86,52 @@ def tile_picked_twqpullbcube_none_p_kernel(
             nc.vector.tensor_copy(got[:], table[:].indirect(lst[:]))
             return got
 
-        def cast_weight(raw, name):
-            wb = sb([P, PACK, P, PACK], BF16, name)
-            for c in range(2):
-                nc.scalar.copy(
-                    wb[:, :, c * 64 : (c + 1) * 64, :].rearrange("p t m j -> p m j t"),
-                    raw[c][:].rearrange("p j (m t) -> p m j t", t=PACK),
-                )
-            return wb
+        def cast_half(wb, raw, c):
+            nc.scalar.copy(
+                wb[:, :, c * 64 : (c + 1) * 64, :].rearrange("p t m j -> p m j t"),
+                raw[c][:].rearrange("p j (m t) -> p m j t", t=PACK),
+            )
+
+        def operand(width, name):
+            return sb([P, width], U32, name + "_codes"), sb([P, width], U8, name + "_scales")
+
+        def quantize_into(dst, cols, src):
+            nc.vector.quantize_mx(out=dst[0][:, cols].bitcast(FP8X4), scales=dst[1][:, cols], in_=src)
 
         def quantize(src, width, name):
-            codes = sb([P, width], U32, name + "_codes")
-            scales = sb([P, width], U8, name + "_scales")
-            nc.vector.quantize_mx(out=codes[:].bitcast(FP8X4), scales=scales[:], in_=src)
-            return codes, scales
+            dst = operand(width, name)
+            quantize_into(dst, slice(0, width), src)
+            return dst
 
-        def product(bank, width, lhs, t, rhs, name):
-            acc = psum.tile([P, width], F32, name=name, tag=f"bank{bank}")
-            cols = slice(t * P, (t + 1) * P)
+        def product(bank, cols, lhs, t, rhs, name):
+            acc = psum.tile([P, cols.stop - cols.start], F32, name=name, tag=f"bank{bank}")
+            rows = slice(t * P, (t + 1) * P)
             nc.tensor.matmul_mx(
                 out=acc[:],
-                lhsT=lhs[0][:, cols].bitcast(FP8X4),
-                lhsT_scale=lhs[1][:, cols],
-                rhs=rhs[0][:].bitcast(FP8X4),
-                rhs_scale=rhs[1][:],
+                lhsT=lhs[0][:, rows].bitcast(FP8X4),
+                lhsT_scale=lhs[1][:, rows],
+                rhs=rhs[0][:, cols].bitcast(FP8X4),
+                rhs_scale=rhs[1][:, cols],
                 start=True,
                 stop=True,
             )
             return acc
 
+        x2s = pick_bytes(xs, l_two, "x2s")
+        x1s = pick_bytes(xs, l_offs, "x1s")
         x2w = pick_words(xw, l_two, "x2w")
         x1w = pick_words(xw, l_offs, "x1w")
-        x2s = pick_bytes(xs, l_two, "x2s")
-        w2b = cast_weight(w2_raw, "w2b")
+        w2b = sb([P, PACK, P, PACK], BF16, "w2b")
+        w1b = sb([P, PACK, P, PACK], BF16, "w1b")
+        cast_half(w2b, w2_raw, 0)
+        cast_half(w2b, w2_raw, 1)
+        cast_half(w1b, w1_raw, 0)
         w2q = quantize(w2b[:].rearrange("p t m j -> p (t m j)"), H, "w2q")
-        x1s = pick_bytes(xs, l_offs, "x1s")
-        d_acc = [product(t, S, w2q, t, (x2w, x2s), f"d_acc{t}") for t in range(PACK)]
+        d_acc = [product(t, slice(0, S), w2q, t, (x2w, x2s), f"d_acc{t}") for t in range(PACK)]
 
-        def evac_d(t, by_dma):
+        def evac_d(t):
             nc.scalar.copy(win_d[t][:, 0:S], d_acc[t][:])
-            if by_dma:
-                nc.sync.dma_start(win_y[t][:, S:WINDOW], win_d[t][:, 0:S])
-            else:
-                nc.scalar.copy(win_y[t][:, S:WINDOW], d_acc[t][:])
+            nc.scalar.copy(win_y[t][:, S:WINDOW], d_acc[t][:])
 
         diff = [sb([P, S], F32, f"diff{t}") for t in range(PACK)]
         gate = [sb([P, S], F32, f"gate{t}") for t in range(PACK)]
@@ -140,28 +141,28 @@ def tile_picked_twqpullbcube_none_p_kernel(
 
         dg_bytes = pick_bytes(ds, l_k1, "dg_bytes")
         dg_words = pick_words(dw, l_k1, "dg_words")
-        evac_d(0, False)
-        evac_d(2, True)
-        evac_d(3, True)
-        evac_d(1, False)
-        w1b = cast_weight(w1_raw, "w1b")
         dealt_bytes = sb([P, H], U8, "dealt_bytes")
         nc.vector.tensor_copy(
             dealt_bytes[:].bitcast(I32).rearrange("p (t a) -> p a t", t=PACK),
             dg_bytes[:].bitcast(I32).rearrange("p (a t) -> p a t", t=PACK),
         )
+        for r in range(4):
+            nc.sync.dma_start(dq_scales[r:P:32, :].bitcast(I32), dealt_bytes[8 * r : P : 32, :].bitcast(I32))
+        evac_d(0)
+        evac_d(1)
+        cast_half(w1b, w1_raw, 1)
+        evac_d(2)
+        evac_d(3)
+        pull_d(0)
         dq_words = sb([P, H], U32, "dq_words")
         nc.vector.tensor_copy(
             dq_words[:].rearrange("p (t a b) -> p a t b", t=PACK, b=4),
             dg_words[:].rearrange("p (a t b) -> p a t b", t=PACK, b=4),
         )
-        for r in range(4):
-            nc.sync.dma_start(dq_scales[r:P:32, :].bitcast(I32), dealt_bytes[8 * r : P : 32, :].bitcast(I32))
-        pull_d(0)
+        w1q = quantize(w1b[:].rearrange("p t m j -> p (t m j)"), H, "w1q")
+        y_acc = [product(4 + t, slice(0, S), w1q, t, (x1w, x1s), f"y_acc{t}") for t in range(PACK)]
         pull_d(1)
         pull_d(2)
-        w1q = quantize(w1b[:].rearrange("p t m j -> p (t m j)"), H, "w1q")
-        y_acc = [product(4 + t, S, w1q, t, (x1w, x1s), f"y_acc{t}") for t in range(PACK)]
         pull_d(3)
 
         for t in range(PACK):
@@ -183,43 +184,55 @@ def tile_picked_twqpullbcube_none_p_kernel(
                 near[c][:, t, :], gate[t][:, cols], 1.0, win_y[t][:, cols], ALU.subtract, ALU.mult
             )
 
-        zb = [sb([P, HALF * PACK], BF16, f"zb{c}") for c in range(2)]
+        zb = sb([P, S * PACK], BF16, "zb")
+        zq = operand(S, "zq")
+        dq = (dq_words, dq_scales)
 
-        def join(c):
+        def join(cols):
+            c = cols.start // HALF
+            part = slice(cols.start - c * HALF, cols.stop - c * HALF)
             nc.vector.tensor_tensor(
-                zb[c][:].rearrange("p (g i t) -> p g t i", i=4, t=PACK),
-                far[c][:].rearrange("p t (g i) -> p g t i", i=4),
-                near[c][:].rearrange("p t (g i) -> p g t i", i=4),
+                zb[:, cols.start * PACK : cols.stop * PACK].rearrange("p (g i t) -> p g t i", i=4, t=PACK),
+                far[c][:, :, part].rearrange("p t (g i) -> p g t i", i=4),
+                near[c][:, :, part].rearrange("p t (g i) -> p g t i", i=4),
                 ALU.subtract,
             )
+
+        def quantize_z(cols):
+            quantize_into(zq, cols, zb[:, cols.start * PACK : cols.stop * PACK])
 
         h_again = [sb([P, S], F32, f"h_again{t}") for t in range(PACK)]
         alpha = math.sqrt(2.0) / 16.0
         beta = math.sqrt(2.0)
 
-        def second_product(c, zq):
-            cols = slice(c * HALF, (c + 1) * HALF)
-            for t in range(PACK):
-                acc = product(2 * t + c, HALF, (dq_words, dq_scales), t, zq, f"h_acc{t}_{c}")
-                nc.scalar.activation(win_d[t][:, cols], acc[:], ACT.Copy, scale=alpha)
-                nc.scalar.activation(h_again[t][:, cols], acc[:], ACT.Copy, scale=alpha)
-                if c == 1:
-                    finish(t)
+        def evac_h(t, cols, acc):
+            nc.scalar.activation(win_d[t][:, cols], acc[:], ACT.Copy, scale=alpha)
+
+        def evac_h_again(t, cols, acc):
+            nc.scalar.activation(h_again[t][:, cols], acc[:], ACT.Copy, scale=alpha)
 
         out_rows = out.rearrange("(a t b) n -> t a b n", t=PACK, b=4)
+        sig = [sb([P, S], F32, f"sig{t}") for t in range(PACK)]
+        pair = [sb([P, S], F32, f"pair{t}") for t in range(PACK)]
 
-        def finish(t):
-            sig = sb([P, S], F32, f"sig{t}")
-            nc.scalar.activation(sig[:], win_d[t][:].indirect(l_n4[:]), ACT.Sigmoid, scale=beta)
-            pair = sb([P, S], F32, f"pair{t}")
-            nc.vector.tensor_tensor(pair[:], win_d[t][:].indirect(l_n3[:]), h_again[t][:], ALU.mult)
-            pieces = 2 if t == PACK - 1 else 1
-            width = S // pieces
-            for c in range(pieces):
-                cols = slice(c * width, (c + 1) * width)
-                res = sb([P, width], F32, f"res{t}_{c}")
-                nc.vector.scalar_tensor_tensor(res[:], sig[:, cols], 0.5, pair[:, cols], ALU.subtract, ALU.mult)
-                nc.sync.dma_start(out_rows[t][:, :, cols], res[:])
+        def squash(t):
+            nc.scalar.activation(sig[t][:], win_d[t][:].indirect(l_n4[:]), ACT.Sigmoid, scale=beta)
+
+        def pair_up(t, cols):
+            nc.vector.tensor_tensor(
+                pair[t][:, cols],
+                win_d[t][:].indirect(l_n3[:, cols.start // 16 : cols.stop // 16]),
+                h_again[t][:, cols],
+                ALU.mult,
+            )
+
+        def finish(t, cols):
+            res = sb([P, cols.stop - cols.start], F32, f"res{t}_{cols.start}")
+            nc.vector.scalar_tensor_tensor(res[:], sig[t][:, cols], 0.5, pair[t][:, cols], ALU.subtract, ALU.mult)
+            nc.sync.dma_start(out_rows[t][:, :, cols], res[:])
+
+        whole, first, second = slice(0, S), slice(0, HALF), slice(HALF, S)
+        third, fourth = slice(HALF, 3 * S // 4), slice(3 * S // 4, S)
 
         for c in range(2):
             far_part(0, c)
@@ -227,14 +240,39 @@ def tile_picked_twqpullbcube_none_p_kernel(
         for t in range(1, PACK):
             far_part(t, 0)
             near_part(t, 0)
-        join(0)
+        join(first)
         far_part(1, 1)
-        zq0 = quantize(zb[0][:], HALF, "zq0")
-        second_product(0, zq0)
+        quantize_z(first)
+        for t in range(PACK):
+            acc = product(t, first, dq, t, zq, f"h_first{t}")
+            evac_h(t, first, acc)
+            evac_h_again(t, first, acc)
         near_part(1, 1)
         for t in range(2, PACK):
             far_part(t, 1)
             near_part(t, 1)
-        join(1)
-        zq1 = quantize(zb[1][:], HALF, "zq1")
-        second_product(1, zq1)
+        join(third)
+        join(fourth)
+        quantize_z(third)
+        quantize_z(fourth)
+        h_third = product(4, third, dq, 0, zq, "h_third")
+        h_fourth = product(0, fourth, dq, 0, zq, "h_fourth")
+        h_second = [None] + [product(4 + t, second, dq, t, zq, f"h_second{t}") for t in range(1, PACK)]
+        evac_h(0, third, h_third)
+        evac_h(0, fourth, h_fourth)
+        evac_h_again(0, third, h_third)
+        evac_h_again(0, fourth, h_fourth)
+        for t in range(2, PACK):
+            evac_h(t, second, h_second[t])
+            nc.sync.dma_start(h_again[t][:, second], win_d[t][:, second])
+        evac_h(1, second, h_second[1])
+        evac_h_again(1, second, h_second[1])
+        pair_up(0, first)
+        pair_up(0, second)
+        for t in range(1, PACK):
+            squash(t - 1)
+            pair_up(t, whole)
+            finish(t - 1, whole)
+        squash(PACK - 1)
+        finish(PACK - 1, slice(0, fourth.start))
+        finish(PACK - 1, fourth)

@@ -20,6 +20,7 @@ P = 128
 PACK = 4
 HALF = S // 2
 WINDOW = 2 * S
+RAW = [P, PACK, H // 2]
 
 
 def tile_picked_twqpullbcube_none_p_kernel(
@@ -28,6 +29,7 @@ def tile_picked_twqpullbcube_none_p_kernel(
     nc = tc.nc
     with ExitStack() as ctx:
         held = ctx.enter_context(tc.tile_pool(name="held", bufs=1))
+        placed = ctx.enter_context(tc.tile_pool(name="placed", bufs=1))
         psum = ctx.enter_context(tc.psum_pool(name="psum", bufs=1))
 
         def sb(shape, dtype, name):
@@ -38,8 +40,7 @@ def tile_picked_twqpullbcube_none_p_kernel(
             nc.sync.dma_start(lst[:], src)
             return lst
 
-        def load_weight_half(w, c, name):
-            raw = sb([P, PACK, H // 2], F32, name)
+        def load_weight_half(w, c, raw):
             nc.sync.dma_start(raw[:], w[:, c * (H // 2) : (c + 1) * (H // 2)].rearrange("(p j) c -> p j c", j=PACK))
             return raw
 
@@ -47,14 +48,12 @@ def tile_picked_twqpullbcube_none_p_kernel(
         nc.gpsimd.memset(xs[:].bitcast(I32), 0)
         ds = sb([P, G], U8, "ds")
         nc.gpsimd.memset(ds[:].bitcast(I32), 0)
+        win_d = [sb([P, WINDOW], F32, f"win_d{t}") for t in range(2)]
+        win_y = [sb([P, WINDOW], F32, f"win_y{t}") for t in range(PACK)]
+        nc.gpsimd.memset(win_d[0][:, S:WINDOW], 0.0)
+        nc.scalar.activation(win_d[1][:, S:WINDOW], win_d[0][:, S:WINDOW], ACT.Sigmoid)
         dq_scales = sb([P, H], U8, "dq_scales")
         nc.gpsimd.memset(dq_scales[:].bitcast(I32), 0)
-        win_d = [sb([P, WINDOW], F32, f"win_d{t}") for t in range(PACK)]
-        win_y = [sb([P, WINDOW], F32, f"win_y{t}") for t in range(PACK)]
-        for t in range(PACK):
-            (nc.vector if t < 2 else nc.gpsimd).memset(win_d[t][:, S:WINDOW], 0.0)
-        warm = sb([P, 8], F32, "warm")
-        nc.scalar.activation(warm[:, 0:1], win_d[0][:, S : S + 1], ACT.Sigmoid)
 
         l_two = load_list(two, "l_two")
         for q in range(4):
@@ -62,13 +61,14 @@ def tile_picked_twqpullbcube_none_p_kernel(
         l_offs = load_list(offs, "l_offs")
         xw = sb([P, T], U32, "xw")
         nc.sync.dma_start(xw[:].bitcast(I32), x_words[0].rearrange("p n t -> p (n t)").bitcast(I32))
-        w2_raw = [load_weight_half(w2, c, f"w2_raw{c}") for c in range(2)]
-        w1_raw = [load_weight_half(w1, 0, "w1_raw0")]
+        w2_raw = [load_weight_half(w2, c, sb(RAW, F32, f"w2_raw{c}")) for c in range(2)]
+        w1_raw = [load_weight_half(w1, 0, sb(RAW, F32, "w1_raw0"))]
         l_k1 = load_list(k1, "l_k1")
         nc.sync.dma_start(ds[0:P:8, :].bitcast(I32), d_scales[0].bitcast(I32))
         dw = sb([P, G], U32, "dw")
         nc.sync.dma_start(dw[:].bitcast(I32), d_words[0].rearrange("p n t -> p (n t)").bitcast(I32))
-        w1_raw.append(load_weight_half(w1, 1, "w1_raw1"))
+        w1_last = placed.tile(RAW, F32, name="w1_raw1", offset=2 * WINDOW)
+        w1_raw.append(load_weight_half(w1, 1, w1_last))
         l_n2 = load_list(n2, "l_n2")
         gain = sb([P, PACK], F32, "gain")
         nc.sync.dma_start(gain[:], gs.rearrange("(p t) o -> p (t o)", t=PACK))
@@ -151,17 +151,21 @@ def tile_picked_twqpullbcube_none_p_kernel(
         evac_d(0)
         evac_d(1)
         cast_half(w1b, w1_raw, 1)
-        evac_d(2)
-        evac_d(3)
+        for t in range(2, PACK):
+            win_d.append(placed.tile([P, WINDOW], F32, name=f"win_d{t}", offset=(t - 2) * 4 * WINDOW))
+            nc.gpsimd.memset(win_d[t][:, S:WINDOW], 0.0)
+            nc.scalar.copy(win_d[t][:, 0:S], d_acc[t][:])
+        for t in range(2, PACK):
+            nc.scalar.copy(win_y[t][:, S:WINDOW], win_d[t][:, 0:S])
         pull_d(0)
         dq_words = sb([P, H], U32, "dq_words")
         nc.vector.tensor_copy(
             dq_words[:].rearrange("p (t a b) -> p a t b", t=PACK, b=4),
             dg_words[:].rearrange("p (a t b) -> p a t b", t=PACK, b=4),
         )
+        pull_d(1)
         w1q = quantize(w1b[:].rearrange("p t m j -> p (t m j)"), H, "w1q")
         y_acc = [product(4 + t, slice(0, S), w1q, t, (x1w, x1s), f"y_acc{t}") for t in range(PACK)]
-        pull_d(1)
         pull_d(2)
         pull_d(3)
 
@@ -169,19 +173,23 @@ def tile_picked_twqpullbcube_none_p_kernel(
             nc.scalar.activation(gate[t][:], diff[t][:], ACT.Sigmoid)
             nc.scalar.activation(win_y[t][:, 0:S], y_acc[t][:], ACT.Copy, scale=gain[:, t : t + 1])
 
-        far = [sb([P, PACK, HALF], F32, f"far{c}") for c in range(2)]
-        near = [sb([P, PACK, HALF], F32, f"near{c}") for c in range(2)]
+        far_slots = sb([P, PACK + 1, HALF], F32, "far_slots")
+        far = [far_slots[:, 1 : PACK + 1, :], far_slots[:, 0:PACK, :]]
+        near = sb([P, PACK, HALF], F32, "near")
 
-        def far_part(t, c):
-            cols = slice(c * HALF, (c + 1) * HALF)
+        def far_part(t, cols):
+            c = cols.start // HALF
             nc.vector.tensor_tensor(
-                far[c][:, t, :], win_y[t][:].indirect(l_n1[:, c * 16 : (c + 1) * 16]), gate[t][:, cols], ALU.mult
+                far[c][:, t, cols.start - c * HALF : cols.stop - c * HALF],
+                win_y[t][:].indirect(l_n1[:, cols.start // 16 : cols.stop // 16]),
+                gate[t][:, cols],
+                ALU.mult,
             )
 
         def near_part(t, c):
             cols = slice(c * HALF, (c + 1) * HALF)
             nc.vector.scalar_tensor_tensor(
-                near[c][:, t, :], gate[t][:, cols], 1.0, win_y[t][:, cols], ALU.subtract, ALU.mult
+                near[:, t, :], gate[t][:, cols], 1.0, win_y[t][:, cols], ALU.subtract, ALU.mult
             )
 
         zb = sb([P, S * PACK], BF16, "zb")
@@ -194,7 +202,7 @@ def tile_picked_twqpullbcube_none_p_kernel(
             nc.vector.tensor_tensor(
                 zb[:, cols.start * PACK : cols.stop * PACK].rearrange("p (g i t) -> p g t i", i=4, t=PACK),
                 far[c][:, :, part].rearrange("p t (g i) -> p g t i", i=4),
-                near[c][:, :, part].rearrange("p t (g i) -> p g t i", i=4),
+                near[:, :, part].rearrange("p t (g i) -> p g t i", i=4),
                 ALU.subtract,
             )
 
@@ -234,23 +242,26 @@ def tile_picked_twqpullbcube_none_p_kernel(
         whole, first, second = slice(0, S), slice(0, HALF), slice(HALF, S)
         third, fourth = slice(HALF, 3 * S // 4), slice(3 * S // 4, S)
 
-        for c in range(2):
-            far_part(0, c)
-            near_part(0, c)
+        far_part(0, first)
+        near_part(0, 0)
+        far_part(0, second)
         for t in range(1, PACK):
-            far_part(t, 0)
+            far_part(t, first)
             near_part(t, 0)
         join(first)
-        far_part(1, 1)
+        near_part(0, 1)
         quantize_z(first)
         for t in range(PACK):
             acc = product(t, first, dq, t, zq, f"h_first{t}")
             evac_h(t, first, acc)
             evac_h_again(t, first, acc)
+        far_part(1, second)
         near_part(1, 1)
-        for t in range(2, PACK):
-            far_part(t, 1)
-            near_part(t, 1)
+        far_part(2, second)
+        near_part(2, 1)
+        near_part(3, 1)
+        far_part(3, third)
+        far_part(3, fourth)
         join(third)
         join(fourth)
         quantize_z(third)

import math
from contextlib import ExitStack

import concourse.mybir as mybir

K, T, S, H, G = 512, 1024, 512, 512, 2048
FLOPS = 3 * 2 * K * H * S

F32 = mybir.dt.float32
BF16 = mybir.dt.bfloat16
I32 = mybir.dt.int32
U32 = mybir.dt.uint32
U16 = mybir.dt.uint16
U8 = mybir.dt.uint8
FP8X4 = mybir.dt.float8_e4m3fn_x4
ACT = mybir.ActivationFunctionType
ALU = mybir.AluOpType

P = 128
PACK = 4
HALF = S // 2
WINDOW = 2 * S
RAW = [P, PACK, H // 2]


def tile_picked_twqpullbcube_none_p_kernel(
    tc, x_words, x_scales, w1, w2, gs, d_words, d_scales, offs, two, n1, n2, k1, n3, n4, out
):
    nc = tc.nc
    with ExitStack() as ctx:
        held = ctx.enter_context(tc.tile_pool(name="held", bufs=1))
        placed = ctx.enter_context(tc.tile_pool(name="placed", bufs=1))
        psum = ctx.enter_context(tc.psum_pool(name="psum", bufs=1))

        def sb(shape, dtype, name):
            return held.tile(shape, dtype, name=name, align_bytes=64)

        def load_list(src, name):
            lst = sb([P, S // 16], U16, name)
            nc.sync.dma_start(lst[:], src)
            return lst

        def load_weight_half(w, c, raw):
            nc.sync.dma_start(raw[:], w[:, c * (H // 2) : (c + 1) * (H // 2)].rearrange("(p j) c -> p j c", j=PACK))
            return raw

        xs = sb([P, T], U8, "xs")
        nc.gpsimd.memset(xs[:].bitcast(I32), 0)
        ds = sb([P, G], U8, "ds")
        nc.gpsimd.memset(ds[:].bitcast(I32), 0)
        win_d = [sb([P, WINDOW], F32, f"win_d{t}") for t in range(2)]
        win_y = [sb([P, WINDOW], F32, f"win_y{t}") for t in range(PACK)]
        nc.gpsimd.memset(win_d[0][:, S:WINDOW], 0.0)
        nc.scalar.activation(win_d[1][:, S:WINDOW], win_d[0][:, S:WINDOW], ACT.Sigmoid)
        dq_scales = sb([P, H], U8, "dq_scales")
        nc.gpsimd.memset(dq_scales[:].bitcast(I32), 0)

        l_two = load_list(two, "l_two")
        for q in range(4):
            nc.sync.dma_start(xs[32 * q : 32 * q + 4, :].bitcast(I32), x_scales[0][4 * q : 4 * q + 4, :].bitcast(I32))
        l_offs = load_list(offs, "l_offs")
        xw = sb([P, T], U32, "xw")
        nc.sync.dma_start(xw[:].bitcast(I32), x_words[0].rearrange("p n t -> p (n t)").bitcast(I32))
        w2_raw = [load_weight_half(w2, c, sb(RAW, F32, f"w2_raw{c}")) for c in range(2)]
        w1_raw = [load_weight_half(w1, 0, sb(RAW, F32, "w1_raw0"))]
        l_k1 = load_list(k1, "l_k1")
        nc.sync.dma_start(ds[0:P:8, :].bitcast(I32), d_scales[0].bitcast(I32))
        dw = sb([P, G], U32, "dw")
        nc.sync.dma_start(dw[:].bitcast(I32), d_words[0].rearrange("p n t -> p (n t)").bitcast(I32))
        w1_last = placed.tile(RAW, F32, name="w1_raw1", offset=2 * WINDOW)
        w1_raw.append(load_weight_half(w1, 1, w1_last))
        l_n2 = load_list(n2, "l_n2")
        gain = sb([P, PACK], F32, "gain")
        nc.sync.dma_start(gain[:], gs.rearrange("(p t) o -> p (t o)", t=PACK))
        l_n1 = load_list(n1, "l_n1")
        l_n3 = load_list(n3, "l_n3")
        l_n4 = load_list(n4, "l_n4")

        def pick_words(table, lst, name):
            got = sb([P, S], U32, name)
            nc.vector.tensor_copy(got[:], table[:].indirect(lst[:]))
            return got

        def pick_bytes(table, lst, name):
            got = sb([P, S], U8, name)
            nc.vector.tensor_copy(got[:], table[:].indirect(lst[:]))
            return got

        def cast_half(wb, raw, c):
            nc.scalar.copy(
                wb[:, :, c * 64 : (c + 1) * 64, :].rearrange("p t m j -> p m j t"),
                raw[c][:].rearrange("p j (m t) -> p m j t", t=PACK),
            )

        def operand(width, name):
            return sb([P, width], U32, name + "_codes"), sb([P, width], U8, name + "_scales")

        def quantize_into(dst, cols, src):
            nc.vector.quantize_mx(out=dst[0][:, cols].bitcast(FP8X4), scales=dst[1][:, cols], in_=src)

        def quantize(src, width, name):
            dst = operand(width, name)
            quantize_into(dst, slice(0, width), src)
            return dst

        def product(bank, cols, lhs, t, rhs, name):
            acc = psum.tile([P, cols.stop - cols.start], F32, name=name, tag=f"bank{bank}")
            rows = slice(t * P, (t + 1) * P)
            nc.tensor.matmul_mx(
                out=acc[:],
                lhsT=lhs[0][:, rows].bitcast(FP8X4),
                lhsT_scale=lhs[1][:, rows],
                rhs=rhs[0][:, cols].bitcast(FP8X4),
                rhs_scale=rhs[1][:, cols],
                start=True,
                stop=True,
            )
            return acc

        x2s = pick_bytes(xs, l_two, "x2s")
        x1s = pick_bytes(xs, l_offs, "x1s")
        x2w = pick_words(xw, l_two, "x2w")
        x1w = pick_words(xw, l_offs, "x1w")
        w2b = sb([P, PACK, P, PACK], BF16, "w2b")
        w1b = sb([P, PACK, P, PACK], BF16, "w1b")
        cast_half(w2b, w2_raw, 0)
        cast_half(w2b, w2_raw, 1)
        cast_half(w1b, w1_raw, 0)
        w2q = quantize(w2b[:].rearrange("p t m j -> p (t m j)"), H, "w2q")
        d_acc = [product(t, slice(0, S), w2q, t, (x2w, x2s), f"d_acc{t}") for t in range(PACK)]

        def evac_d(t):
            nc.scalar.copy(win_d[t][:, 0:S], d_acc[t][:])
            nc.scalar.copy(win_y[t][:, S:WINDOW], d_acc[t][:])

        diff = [sb([P, S], F32, f"diff{t}") for t in range(PACK)]
        gate = [sb([P, S], F32, f"gate{t}") for t in range(PACK)]

        def pull_d(t):
            nc.vector.tensor_tensor(diff[t][:], win_d[t][:].indirect(l_n2[:]), win_y[t][:, S:WINDOW], ALU.subtract)

        dg_bytes = pick_bytes(ds, l_k1, "dg_bytes")
        dg_words = pick_words(dw, l_k1, "dg_words")
        dealt_bytes = sb([P, H], U8, "dealt_bytes")
        nc.vector.tensor_copy(
            dealt_bytes[:].bitcast(I32).rearrange("p (t a) -> p a t", t=PACK),
            dg_bytes[:].bitcast(I32).rearrange("p (a t) -> p a t", t=PACK),
        )
        for r in range(4):
            nc.sync.dma_start(dq_scales[r:P:32, :].bitcast(I32), dealt_bytes[8 * r : P : 32, :].bitcast(I32))
        evac_d(0)
        evac_d(1)
        cast_half(w1b, w1_raw, 1)
        for t in range(2, PACK):
            win_d.append(placed.tile([P, WINDOW], F32, name=f"win_d{t}", offset=(t - 2) * 4 * WINDOW))
            nc.gpsimd.memset(win_d[t][:, S:WINDOW], 0.0)
            nc.scalar.copy(win_d[t][:, 0:S], d_acc[t][:])
        for t in range(2, PACK):
            nc.scalar.copy(win_y[t][:, S:WINDOW], win_d[t][:, 0:S])
        pull_d(0)
        dq_words = sb([P, H], U32, "dq_words")
        nc.vector.tensor_copy(
            dq_words[:].rearrange("p (t a b) -> p a t b", t=PACK, b=4),
            dg_words[:].rearrange("p (a t b) -> p a t b", t=PACK, b=4),
        )
        pull_d(1)
        w1q = quantize(w1b[:].rearrange("p t m j -> p (t m j)"), H, "w1q")
        y_acc = [product(4 + t, slice(0, S), w1q, t, (x1w, x1s), f"y_acc{t}") for t in range(PACK)]
        pull_d(2)
        pull_d(3)

        for t in range(PACK):
            nc.scalar.activation(gate[t][:], diff[t][:], ACT.Sigmoid)
            nc.scalar.activation(win_y[t][:, 0:S], y_acc[t][:], ACT.Copy, scale=gain[:, t : t + 1])

        far_slots = sb([P, PACK + 1, HALF], F32, "far_slots")
        far = [far_slots[:, 1 : PACK + 1, :], far_slots[:, 0:PACK, :]]
        near = sb([P, PACK, HALF], F32, "near")

        def far_part(t, cols):
            c = cols.start // HALF
            nc.vector.tensor_tensor(
                far[c][:, t, cols.start - c * HALF : cols.stop - c * HALF],
                win_y[t][:].indirect(l_n1[:, cols.start // 16 : cols.stop // 16]),
                gate[t][:, cols],
                ALU.mult,
            )

        def near_part(t, c):
            cols = slice(c * HALF, (c + 1) * HALF)
            nc.vector.scalar_tensor_tensor(
                near[:, t, :], gate[t][:, cols], 1.0, win_y[t][:, cols], ALU.subtract, ALU.mult
            )

        zb = sb([P, S * PACK], BF16, "zb")
        zq = operand(S, "zq")
        dq = (dq_words, dq_scales)

        def join(cols):
            c = cols.start // HALF
            part = slice(cols.start - c * HALF, cols.stop - c * HALF)
            nc.vector.tensor_tensor(
                zb[:, cols.start * PACK : cols.stop * PACK].rearrange("p (g i t) -> p g t i", i=4, t=PACK),
                far[c][:, :, part].rearrange("p t (g i) -> p g t i", i=4),
                near[:, :, part].rearrange("p t (g i) -> p g t i", i=4),
                ALU.subtract,
            )

        def quantize_z(cols):
            quantize_into(zq, cols, zb[:, cols.start * PACK : cols.stop * PACK])

        h_again = [sb([P, S], F32, f"h_again{t}") for t in range(PACK)]
        alpha = math.sqrt(2.0) / 16.0
        beta = math.sqrt(2.0)

        def evac_h(t, cols, acc):
            nc.scalar.activation(win_d[t][:, cols], acc[:], ACT.Copy, scale=alpha)

        def evac_h_again(t, cols, acc):
            nc.scalar.activation(h_again[t][:, cols], acc[:], ACT.Copy, scale=alpha)

        out_rows = out.rearrange("(a t b) n -> t a b n", t=PACK, b=4)
        sig = [sb([P, S], F32, f"sig{t}") for t in range(PACK)]
        pair = [sb([P, S], F32, f"pair{t}") for t in range(PACK)]

        def squash(t):
            nc.scalar.activation(sig[t][:], win_d[t][:].indirect(l_n4[:]), ACT.Sigmoid, scale=beta)

        def pair_up(t, cols):
            nc.vector.tensor_tensor(
                pair[t][:, cols],
                win_d[t][:].indirect(l_n3[:, cols.start // 16 : cols.stop // 16]),
                h_again[t][:, cols],
                ALU.mult,
            )

        def finish(t, cols):
            res = sb([P, cols.stop - cols.start], F32, f"res{t}_{cols.start}")
            nc.vector.scalar_tensor_tensor(res[:], sig[t][:, cols], 0.5, pair[t][:, cols], ALU.subtract, ALU.mult)
            nc.sync.dma_start(out_rows[t][:, :, cols], res[:])

        whole, first, second = slice(0, S), slice(0, HALF), slice(HALF, S)
        third, fourth = slice(HALF, 3 * S // 4), slice(3 * S // 4, S)

        far_part(0, first)
        near_part(0, 0)
        far_part(0, second)
        for t in range(1, PACK):
            far_part(t, first)
            near_part(t, 0)
        join(first)
        near_part(0, 1)
        quantize_z(first)
        for t in range(PACK):
            acc = product(t, first, dq, t, zq, f"h_first{t}")
            evac_h(t, first, acc)
            evac_h_again(t, first, acc)
        far_part(1, second)
        near_part(1, 1)
        far_part(2, second)
        near_part(2, 1)
        near_part(3, 1)
        far_part(3, third)
        far_part(3, fourth)
        join(third)
        join(fourth)
        quantize_z(third)
        quantize_z(fourth)
        h_third = product(4, third, dq, 0, zq, "h_third")
        h_fourth = product(0, fourth, dq, 0, zq, "h_fourth")
        h_second = [None] + [product(4 + t, second, dq, t, zq, f"h_second{t}") for t in range(1, PACK)]
        evac_h(0, third, h_third)
        evac_h(0, fourth, h_fourth)
        evac_h_again(0, third, h_third)
        evac_h_again(0, fourth, h_fourth)
        for t in range(2, PACK):
            evac_h(t, second, h_second[t])
            nc.sync.dma_start(h_again[t][:, second], win_d[t][:, second])
        evac_h(1, second, h_second[1])
        evac_h_again(1, second, h_second[1])
        pair_up(0, first)
        pair_up(0, second)
        for t in range(1, PACK):
            squash(t - 1)
            pair_up(t, whole)
            finish(t - 1, whole)
        squash(PACK - 1)
        finish(PACK - 1, slice(0, fourth.start))
        finish(PACK - 1, fourth)
